import numpy as np, ml_dtypes
CORES = [8,9,10,11,12,13]
N = 6
BF = ml_dtypes.bfloat16
def gentries(a):
    return np.ascontiguousarray(a.reshape(8, 16, -1).transpose(0, 2, 1)).reshape(8, -1)
def gtable(e):
    e = np.asarray(e); return np.ascontiguousarray(e.reshape(8, -1, 16).transpose(0, 2, 1)).reshape(128, -1).astype(np.int32)
V, G, Q, LN, CAP, RO = 2048, 1024, 2, 192, 32, 5
W = V + Q * G
def ghosts(a):
    return np.concatenate([a] + [np.roll(a, -d, axis=0)[..., :G] for d in range(1, Q + 1)], axis=-1)
def lists(rng, cl, share):
    cw = ghosts(cl); out = np.zeros((N, 8, 16, V), np.int64)
    for a in range(N):
        for g in range(8):
            c = cw[a, g]; o = np.argsort(c + rng.random(W)); cnt = np.bincount(c); s = np.add.accumulate(cnt) - cnt; m = cl[a, g]
            y = o[s[m] + (rng.random((16, V)) * cnt[m]).astype(np.int64)]
            out[a, g] = np.where(rng.random((16, V)) < share, rng.integers(0, W, (16, V)), y)
    return out
def front(rng, x, l, share):
    xw = ghosts(x).astype(np.int16)
    for a in range(N):
        for g in range(8):
            y = l[a, g]; e = np.sum(np.abs(xw[a, g][:, y] - xw[a, g][:, None, :V]), axis=0)
            k = np.argmin(np.where(y == np.arange(V), 9999, e), axis=0); w = np.nonzero(rng.random(V) < share[a, g])[0]
            old = y[0, w].copy(); y[0, w] = y[k[w], w]; y[k[w], w] = old
    return l
def parts(rng):
    kc = W // 24; cl = rng.integers(0, kc, (N, 8, V)); cen = rng.integers(0, 256, (8, kc, 16))
    x = cen[np.arange(8)[None, :, None], cl].transpose(0, 1, 3, 2) + rng.integers(-24, 25, (N, 8, 16, V))
    return np.clip(x, 0, 255), lists(rng, cl, 0.12)
def pack(x, l, p, th):
    return {"feat": np.ascontiguousarray(x.reshape(N, 128, V)).astype(np.float32).astype(BF), "hits": np.ascontiguousarray(l.reshape(N, 128, V)).astype(np.int32),
            "lane0": np.stack([gtable(a) for a in p]), "th": np.ascontiguousarray(np.reshape(th, (N, 8, 1))).astype(np.int32)}
def setup_inputs(rng):
    x, l = parts(rng); l = front(rng, x, l, rng.choice(np.array([0.3, 0.6, 0.9]), (N, 8)))
    return pack(x, l, rng.integers(0, V, (N, 8, LN)), rng.integers(60, 400, (N, 8)))
def setup_inputs_ends(rng):
    e = np.array([0, W - 1]); x = 255 * rng.integers(0, 2, (N, 8, 16, V)); x[:, 1::2] = x[:, 1::2, :1].copy()
    x[:, 1::2, :, 0] = 0; x[:, 1::2, :, G - 1] = 0; x[:, 1::2, :, G] = 0; x[:, 1::2, :, V - 4:] = 255
    l = np.zeros((N, 8, 16, V), np.int64); p = np.zeros((N, 8, LN), np.int64); k = 3 * LN // 5 + 1; n = LN - k - 3
    for a in range(N):
        for g in range(8):
            o = np.sort(rng.permutation(np.setdiff1d(np.arange(1, V - 4), np.array([G - 1, G])))[:2 * n].reshape(n, 2), axis=1)
            v = np.append(o[:, 0], V - 2); b = np.append(o[:, 1], V - 1); xx = x[a, g]
            if g % 2 == 1: xx[:, v] = 255
            xx[:, b] = xx[:, v]
            y = np.where(rng.random((16, V)) < 0.7, rng.choice(e, (16, V)), rng.integers(0, W, (16, V)))
            y[:, v] = rng.choice(e, (16, n + 1)); y[:, b] = rng.choice(e, (16, n + 1))
            y[rng.integers(0, 15, n + 1), v] = b; y[0, b] = v; y[15, V - 2] = W - 1; y[15, V - 1] = W - 1
            y[:, V - 3] = rng.choice(e, 16); y[0, V - 3] = W - 1; y[15, V - 3] = 0
            y[:, V - 4] = W - 1; y[7, V - 4] = G; y[15, V - 4] = G - 1
            l[a, g] = y
            p[a, g] = np.concatenate([rng.permutation(np.concatenate([rng.choice(np.array([0, V - 1]), k), o[:, 0]])), np.array([V - 4, V - 3, V - 2])])
    return pack(x, l, p, np.stack([rng.permutation(np.array([0, 4080] * 4)) for a in range(N)]))
def setup_inputs_corners(rng):
    x = rng.integers(0, 256, (N, 8, 16, V)); l = np.zeros((N, 8, 16, V), np.int64); p = np.zeros((N, 8, LN), np.int64)
    half = G // 2; me = np.arange(V); p1 = LN // 2; p2 = LN // 8
    for a in range(N):
        for g in range(8):
            even = g % 2 == 0; n = int(rng.choice(np.array([0, 1, CAP - 1, CAP, CAP + 1, p1])))
            if a == 0: n = (CAP, CAP + 1, p1, CAP - 1, 1, 0, CAP, CAP + 1)[g]
            u = G + 1 + rng.permutation(V - G - 2)[:2 * p2]
            if even: u[0] = G
            u = np.sort(u)
            lo = rng.permutation(half)[:p1]; hi = rng.permutation(np.setdiff1d(np.arange(half, V - 1), np.append(u, np.array([G - 1, G]))))[:p1]
            if even:
                lo[0] = G - 1; hi[0] = V - 1
            else:
                hi[0] = G - 1; hi[1] = G
            v = np.concatenate([lo, u[0::2]]); b = np.concatenate([hi, u[1::2]])
            rest = np.setdiff1d(me, np.concatenate([v, b]))
            y = np.where(rng.random((16, V)) < 0.5, (rng.random((16, V)) * me).astype(np.int64), rng.integers(V, W, (16, V)))
            y = np.where(rng.random(V) < 0.0625, me, y)
            z = rest[rng.random(rest.size) < 0.5]; y[rng.integers(0, 8, z.size), z] = V + G - 1
            if Q > 1:
                z = rest[rng.random(rest.size) < 0.5]; y[rng.integers(8, 16, z.size), z] = V + G
            y[:, v] = rng.integers(V, W, (16, v.size)); y[:, b] = rng.integers(V, W, (16, v.size))
            r = rng.integers(0, 16, v.size)
            if even: r[0] = 1 + r[0] % 15
            y[r, v] = b; y[0, b] = v
            if even:
                y[0, v[0]] = rng.integers(0, G - 1); y[r[0], b[0]] = rng.integers(0, G - 1)
            l[a, g] = y
            xx = x[a, g]; xx[:, b] = xx[:, v]
            f = rng.integers(0, 16, v.size); s = rng.integers(2, 4, v.size); xx[f, b] += np.where(xx[f, b] < 128, s, -s)
            w = rng.choice(rest, LN - n - p2)
            if g == 7: w[:] = rest[-1]
            o = np.concatenate([lo[:n], u[0::2], w]); k = 2 if n >= 2 and not even else 0
            p[a, g] = np.concatenate([o[:k], rng.permutation(o[k:])])
    return pack(x, l, p, rng.choice(np.array([0, 1, 200, 4079, 4080]), (N, 8)))
def setup_inputs_trees(rng):
    x, l = parts(rng); p = np.zeros((N, 8, LN), np.int64); j = np.arange(16)
    th = rng.choice(np.array([0, 100, 500, 4080]), (N, 8)); th[:, 1] = rng.choice(np.array([0, 100, 500]), N)
    at = 2 * (j & 1) + 8 * ((j >> 1) & 1) + 32 * ((j >> 2) & 1) + 128 * ((j >> 3) & 1)
    for a in range(N):
        for g in (0, 1, 3, 4, 5, 7):
            n = LN // 16 if g % 2 == 0 else LN // 32; k = 8 * (g % 2); c = rng.permutation(V)
            o = np.sort(c[:16 * n].reshape(n, 16), axis=1); xx, y = x[a, g], l[a, g]
            for i in range(n):
                xx[:, o[i]] = rng.integers(0, 86, (16, 1)) + at[None, :]
                y[:, o[i]] = rng.permutation(o[i])[:, None]
            s = np.sort(c[16 * n:16 * n + 3 * k].reshape(k, 3), axis=1); u, b, w = s[:, 0], s[:, 1], s[:, 2]
            xx[:, b] = xx[:, u] ^ 128; y[:, u] = b; y[:, b] = u; y[:, w] = b
            p[a, g] = rng.permutation(np.concatenate([o.reshape(-1), b, w, rng.integers(0, V, LN - 16 * n - 2 * k)]))
    for g in (2, 6):
        th[:, g] = np.where((np.arange(N) + g // 4) % 2 == 0, 4080, rng.integers(1000, 1500, N))
        x[:, g] = rng.integers(0, 256, (N, 16, V)); pr = np.zeros((N, 2 * CAP, 2), np.int64)
        for a in range(N): pr[a] = np.sort(rng.permutation(G - 1)[:4 * CAP].reshape(2 * CAP, 2), axis=1)
        for a in range(N):
            u, b = pr[a, :, 0], pr[a, :, 1]; xx, y = x[a, g], l[a, g]
            o = rng.permutation(np.setdiff1d(np.arange(V), np.concatenate([u, b, np.array([G - 1, G])]))); w = o[:CAP]; s = o[CAP:LN - 2 * CAP]
            xx[:, b] = np.clip(xx[:, u] + rng.integers(-8, 9, (16, 2 * CAP)), 0, 255)
            y[:, u] = b; y[:, b] = rng.choice(np.array([G - 1, G]), (16, 2 * CAP)); y[0, b] = u; y[:, w] = u[:CAP]
            d = rng.integers(0, Q, (16, s.size)); m = pr[(a + 1 + d) % N, rng.integers(0, 2 * CAP, d.shape), rng.integers(0, 2, d.shape)]
            y[:, s] = V + d * G + np.where(rng.random(d.shape) < 0.75, m, rng.integers(0, G, d.shape))
            p[a, g] = rng.permutation(np.concatenate([b, w, s]))
    return pack(x, l, p, th)
def setup_inputs_ties(rng):
    x = np.full((N, 8, 16, V), 100); x[:, :, 3] += rng.integers(0, 3, (N, 8, V)); x[:, :, 12] += rng.integers(0, 3, (N, 8, V))
    x[..., :] += rng.integers(0, 156 - 2, (N, 8, 1, 1)) * rng.integers(0, 2, (N, 8, 1, V))
    l = lists(rng, rng.integers(0, W // 24, (N, 8, V)), 0.1); l[:, ::2, 8:] = l[:, ::2, :8].copy()
    l = front(rng, x, l, np.full((N, 8), 0.6))
    p = rng.integers(0, V, (N, 8, LN)); p[:, 1::4] = rng.integers(0, 64, (N, 2, LN)); p[:, 3] = V - 1 - rng.integers(0, 128, (N, LN))
    th = rng.integers(0, 5, (N, 8)); th[:, 6] = 2049 + 2 * rng.integers(0, 1016, N); th[:, 7] = rng.choice(np.array([2049, 2051, 4077, 4079]), N)
    for a in range(N):
        for g in (6, 7):
            m = 4 * rng.permutation(V // 4)[:8]; o = rng.permutation(np.setdiff1d(np.arange(V), np.concatenate([m, m + 1])))[:72]
            n = o[:32]; s = np.sort(o[32:64].reshape(16, 2), axis=1); v, b = s[:, 0], s[:, 1]; xx, y = x[a, g], l[a, g]; t = int(th[a, g])
            xx[:, o[:64]] = 0; xx[:, m] = 128; xx[:, m + 1] = 128
            xx[:, o[64:68]] = ((t + np.arange(16)) // 16)[:, None]; xx[:, o[68:72]] = ((t + 1 + np.arange(16)) // 16)[:, None]
            j = rng.integers(0, 8, 32); y[:, n] = o[64 + rng.integers(0, 8, (16, 32))]; y[0, n] = m[j] + 1; y[15, n] = m[j]
            j = rng.integers(0, 8, 16); y[:, v] = m[j] + 1; y[:, b] = m[j]; y[0, v] = b; y[0, b] = v
            p[a, g] = rng.permutation(np.concatenate([n, v, rng.integers(0, V, LN - 48)]))
    return pack(x, l, p, th)
def setup_inputs_spread(rng):
    x = np.minimum((np.exp2(8 * rng.random((N, 8, 1, V))) * rng.random((N, 8, 16, V))).astype(np.int64), 255)
    l = lists(rng, ((W // 16) * rng.random((N, 8, V)) ** 2).astype(np.int64), 0.1); l = front(rng, x, l, rng.choice(np.array([0.5, 1.0]), (N, 8)))
    return pack(x, l, (V * rng.random((N, 8, LN)) ** 1.5).astype(np.int64), (4081 * rng.random((N, 8)) ** 2).astype(np.int64))
def check_inputs(d):
    bad = []
    for k, lo, hi in (("feat", 0, 255), ("hits", 0, W - 1), ("lane0", 0, V - 1), ("th", 0, 4080)):
        v = np.asarray(d[k]).astype(np.float64)
        if not (np.min(v) >= lo and np.max(v) <= hi): bad.append("range of " + k)
        elif np.any(v != np.floor(v)): bad.append("whole numbers of " + k)
    return bad
def at_names(tab, names):
    return np.take_along_axis(tab, names.reshape(N, 8, -1), 2).reshape(names.shape)
def far(x, names, y):
    s = np.zeros(names.shape, np.int64)
    for f in range(16): s += np.abs(at_names(x[:, :, f], names) - y[:, :, f][:, :, None, :])
    return s
def reference(feat, hits, lane0, th):
    x = ghosts(feat.astype(np.float32).astype(np.int64).reshape(N, 8, 16, V)); l = ghosts(hits.astype(np.int64).reshape(N, 8, 16, V))
    t = th.astype(np.int64).reshape(N, 8, 1, 1); p = np.stack([gentries(a) for a in lane0]).astype(np.int64)
    for d in range(1, Q + 1):
        off = V + (d - 1) * G; h = l[..., off:off + G]
        l[..., off:off + G] = np.where(h < G, off + h, off + np.arange(G))
    fw = np.tile(np.arange(W), (N, 8, 1)); best = l[:, :, 0, :V].copy()
    lower = np.arange(LN)[None, :] < np.arange(LN)[:, None]
    for rnd in range(RO):
        v = p; awake = ~np.any((v[..., :, None] == v[..., None, :]) & lower, axis=3)
        v4 = v[:, :, None, :]
        c = at_names(fw, np.take_along_axis(l, v4, 3)); xv = np.take_along_axis(x, v4, 3)
        e = np.where(c == v4, 4096, far(x, c, xv))
        b = np.min(e * 4096 + c, axis=2) & 4095; b4 = b[:, :, None, :]
        a, g, i = np.nonzero(awake); best[a, g, v[a, g, i]] = b[a, g, i]
        own = b < V
        back = at_names(fw, at_names(best, np.minimum(b, V - 1)))
        join = awake & own & (b > v) & (back == v)
        o = at_names(fw, np.take_along_axis(l, b4, 3)); xn = (xv + np.take_along_axis(x, b4, 3)) >> 1
        kc = np.where((c == v4) | (c == b4), 4096 * 4096 + v4, far(x, c, xn) * 4096 + c)
        ko = np.where((o == v4) | (o == b4), 4096 * 4096 + v4, far(x, o, xn) * 4096 + o)
        nl = np.where(join[:, :, None, :], np.minimum(kc, ko) & 4095, np.where(e > t, o, c))
        ct = c[:, :, rnd]
        to = np.where(join, v, np.where(own, b, np.where(ct < V, ct, v)))
        p = np.where(awake, to, v)
        a, g, i = np.nonzero(awake)
        l[a, g, :, v[a, g, i]] = nl[a, g, :, i]
        a, g, i = np.nonzero(join); x[a, g, :, v[a, g, i]] = xn[a, g, :, i]; fw[a, g, b[a, g, i]] = v[a, g, i]
        tell = join & (v < G); cnt = np.add.accumulate(tell.astype(np.int64), axis=2); tell = tell & (cnt <= CAP)
        a, g, i = np.nonzero(tell); m = v[a, g, i]; w = b[a, g, i]; y = nl[a, g, :, i]
        for d in range(1, Q + 1):
            off = V + (d - 1) * G; q = (a - d) % N
            x[q, g, :, off + m] = xn[a, g, :, i]; l[q, g, :, off + m] = np.where(y < G, off + y, (off + m)[:, None])
            s = w < G; fw[q[s], g[s], off + w[s]] = off + m[s]
        fw = np.take_along_axis(fw, fw, 2); p = at_names(fw, p)
    return {"yx": x[..., :V].reshape(N, 128, V).astype(np.float32).astype(BF), "yl": l[..., :V].reshape(N, 128, V).astype(np.float32), "yf": fw[..., :V].astype(np.float32)}

from concourse.bass import DstId, RemoteDMATransfer
from concourse.mybir import AluOpType as AL, AxisListType, ActivationFunctionType as AF

ND = "float16"
RO, NCH, CL = 5, 3, 64
WT = 5248
BIG = float(2 ** 24)
BF, F32, I32, U16 = "bfloat16", "float32", "int32", "uint16"

SCRATCH = {}
for _d, _l in (
        (BF, "X:5248 FH:5248 LO:256 Fg:3072 Gc:3072 Go:3072 A1:3072 A2:3072 A3:3072 E:2304 CG:768 TRI:2048 TA:1024 FT:2048 "
             "Z4:144 Z8:144 ZF:144 BO1:128 BO4:128 BOF:128 I1:128 IH:128 IB:128 IM:128 IX:128 CK:64 CQ:64 C128:64 ONE:192 "
             "pHL:384 bk:192 GH:64 xv:192 xb:192 zS:208 fl:1344 junk:192 cS:192 jk:384"),
        (F32, "L:5248 YF:2048 NI:1024 Y0:1024 Y1:1024 Y2:1024 J:160 Jg:128 col:64 LT:16 EQ:16 I32:128 IW0:160 IW1:160 RST:64 "
              "dum:12 slot:24 PB:416 pI:24 KT:192 KS:192 t1:192 bR:208 o:400 m:160 M1:144 M2:128 LA1:288 LA2:256"),
        (I32, "H:4320 lane:12 th1:8 thb:8 pc:2 n0:192 nl:208 KI:384"),
        (U16, "LOG:200 PAR:80 GJ:16 GP:16 FU:128 lvU:192 cU:192 lbU:192 oU:192 sU:64"),
        (ND, "SELT:2048 ZT:864 IN:128 I4:128 cN:384 oN:192 sN:192 BgN:192 vbN:64 oR:60")):
    for _x in _l.split():
        SCRATCH[_x.split(":")[0]] = ("sbuf", [128, int(_x.split(":")[1])], _d)
for _n in ("qA0", "qA1", "qK0", "qK1", "qP", "qZ", "qS", "qR"):
    SCRATCH[_n] = ("psum", [128, 512], F32)

SZ = {BF: 2, F32: 4, I32: 4, U16: 2, ND: 2}
MODEL = (1.0, 1.0, 1.55, 3.8, 0.5, 120.0, 80.0, 1.0)
ENG = ("pe", "dve", "act", "pool", "sp")
SLACK = 60.0


def keys():
    ks = []
    for t in range(RO):
        for ch in range(NCH):
            ks += [((t, A, ch), "dve") for A in ("A1", "A2", "A3")]
            ks += [((t, G, ch, h), "act") for G in ("Gc", "Go", "FcU", "FoU") if t or G[0] == "G" for h in range(2)]
            ks += [((t, "xb", ch), "act"), ((t, "sg", ch), "act")]
        ks += [((t, "xv"), "act"), ((t, "bk"), "dve"), ((t, "to"), "dve")]
        if t < RO - 1:
            ks += [((t, "sn", k), "act") for k in range(2)] + [((t, "cg", s), "act") for s in range(t)]
    return ks + [((RO - 1, "fu", h), "act") for h in range(4)]


def choice(h):
    return {k: ({"act": "dve", "dve": "act"}[d] if b == "1" else d) for (k, d), b in zip(keys(), bin(h)[3:])}


CFG = choice(0x11190d00e00940000476008b8028a0ac183e019082c012200101140)
NOISE = {1177: -4000, 771: -3000, 125: -1000, 563: -3000, 1069: 1000, 1320: -3000, 888: 1000, 852: -400, 187: -400, 756: 3000,
         289: 3000, 471: -400, 250: 400, 836: -400, 481: 3000, 1038: 3000, 965: -400, 338: 400, 703: -400, 652: 1000, 1168: 400,
         30: -400, 85: -400, 614: 400, 23: 1000, 91: 3000, 117: 1000, 529: -400, 412: 3000, 938: -400, 175: -400}


def v(n, a, b=None, s=1, p=None):
    return (n, a, a + 1 if b is None else b, s, p)


def ind(w, o):
    return ("*", w, o)


def cnt(x):
    if x[0] == "*":
        return 16 * cnt(x[2])
    return (x[2] - x[1] + x[3] - 1) // x[3]


def dty(x):
    return SCRATCH[(x[1] if x[0] == "*" else x)[0]][2]


def isps(x):
    return x[0] != "*" and SCRATCH[x[0]][0] == "psum"


def ap(T, x):
    if not isinstance(x, tuple):
        return x
    if x[0] == "*":
        return ap(T, x[1]).indirect(ap(T, x[2]))
    p = x[4] or (0, 128)
    cs = slice(x[1], x[2]) if x[3] == 1 else slice(x[1], x[2], x[3])
    return T[x[0]][p[0]:p[1], cs]


def regs(xs):
    out = []
    for x in xs:
        if isinstance(x, tuple):
            out += [x[1][:3], x[2][:3]] if x[0] == "*" else [x[:3]]
    return out


def build(cfg):
    ops, hist = [], {}
    eng_of = lambda k, dflt: cfg.get(k, dflt)

    def add(eng, ins, rd, wr, dur, kind="c", sem=None, lat=0.0, after=()):
        i = len(ops)
        dur = dur if isinstance(dur, tuple) else (dur, 0, 0, 0, 0)
        deps = set(after)
        for rs, w in ((rd, False), (wr, True)):
            for (n, a, b) in rs:
                for (a2, b2, j, w2) in hist.get(n, []):
                    if a2 < b and a < b2 and (w or w2):
                        deps.add(j)
        for (n, a, b) in wr:
            hist[n] = [h for h in hist.get(n, []) if not (a <= h[0] and h[1] <= b)] + [(a, b, i, True)]
        for (n, a, b) in set(rd):
            hist.setdefault(n, []).append((a, b, i, False))
        banks = set(n for (n, a, b) in rd + wr if n in SCRATCH and SCRATCH[n][0] == "psum")
        ops.append({"eng": eng, "ins": ins, "deps": deps, "dur": dur, "kind": kind, "sem": sem, "lat": lat,
                    "banks": banks, "tag": wr[0][0] if wr else "-"})
        return i

    def io(out, ins):
        if out[0] == "*":
            return regs(ins) + [out[2][:3]], [out[1][:3]]
        return regs(ins), [out[:3]]

    def vcost(out, ins, per, base=50.0):
        n = cnt(out)
        if out[0] == "*":
            return (base, 0, 0, n, 0)
        if ins[0][0] == "*":
            return (base, 0, n, 0, 0)
        return (base - 50.0, max(64.0, n * per), 0, 0, 0)

    def half(out, ins):
        return 0.5 if all(SZ[dty(x)] == 2 for x in [out] + ins) else 1.0

    def cp(out, a):
        return (lambda q, T, c: q.tensor_copy(ap(T, out), ap(T, a)),) + io(out, [a]) + (vcost(out, [a], half(out, [a])),)

    def tr(out, a):
        return (lambda q, T, c: q.transpose(ap(T, out), ap(T, a)),) + io(out, [a]) + (vcost(out, [a], 1.0),)

    def tt(out, a, b, op):
        per = 1.0 if isps(a) or isps(b) else 2.0
        return (lambda q, T, c: q.tensor_tensor(ap(T, out), ap(T, a), ap(T, b), op),) + io(out, [a, b]) + (vcost(out, [a], per),)

    def ts(out, a, s1, op0, s2=None, op1=None):
        if op1 is None:
            f = lambda q, T, c: q.tensor_scalar(ap(T, out), ap(T, a), ap(T, s1), None, op0)
        else:
            f = lambda q, T, c: q.tensor_scalar(ap(T, out), ap(T, a), ap(T, s1), ap(T, s2), op0, op1)
        return (f,) + io(out, [a, s1, s2]) + (vcost(out, [a], half(out, [a])),)

    def scan(out, a, b, init, op0, op1):
        f = lambda q, T, c: q.tensor_tensor_scan(ap(T, out), ap(T, a), ap(T, b), init, op0, op1)
        return (f,) + io(out, [a, b]) + (vcost(out, [a], half(out, [a, b])),)

    def mset(out, val):
        return (lambda q, T, c: q.memset(ap(T, out), val),) + io(out, []) + ((0, max(64.0, cnt(out) * SZ[dty(out)] / 4.0), 0, 0, 0),)

    def macro(eng, items, extra_w=()):
        return add(eng, [x[0] for x in items], [r for x in items for r in x[1]],
                   [r for x in items for r in x[2]] + list(extra_w), tuple(sum(x[3][k] for x in items) for k in range(5)))

    def V(*items):
        return macro("dve", items)

    def act(out, a, func=AF.Copy, bias=None, scale=None, acc=None):
        kw = {k: x for k, x in (("bias", bias), ("scale", scale), ("accum_out", acc)) if x is not None}
        rd, wr = io(out, [a, bias, scale])
        f = lambda q, T, c: q.activation(ap(T, out), ap(T, a), func, **{k: ap(T, x) for k, x in kw.items()})
        return macro("act", [(f, rd, wr + regs([acc]), vcost(out, [a], 1.0, 85.0))])

    def gather(eng, out, w, o):
        return act(out, ind(w, o)) if eng == "act" else V(cp(out, ind(w, o)))

    def mm(out, l, r, start, stop):
        c = max(min(64, cnt(l)), cnt(r)) * (4 if dty(r) == F32 else 1)
        return (lambda q, T, c_: q.matmul(ap(T, out), ap(T, l), ap(T, r), start, stop), regs([l, r]), [out[:3]], (0, 0, 0, 0, c))

    def P(items, tok=False):
        return macro("pe", items, [("tok" + items[0][2][0][0], 0, 1)] if tok else [])

    def zs(z, k, base=0):
        return v(z, base + 15 - k, base + 143 - k)

    def diag(out, z, src, a, n, base=0):
        return P([mm(out, zs(z, r, base), v(src, a + r, a + n, 16), r == 0, r == 15) for r in range(16)])

    def spread(bank, a, src, n):
        return P([mm(v(bank, a + r, a + 16 * n, 16), v("SELT", 128 * r, 128 * r + 128), src, True, True) for r in range(16)])

    def pool(f, rd, wr, dur):
        return add("pool", [f], regs(rd), regs(wr), dur)

    def iota(out, pat, base, cm):
        if dty(out) == I32:
            f = lambda q, T, c: q.iota(ap(T, out), pat, base, cm)
        else:
            f = lambda q, T, c: q.iota(ap(T, out), pat, base, cm, allow_small_or_imprecise_dtypes=True)
        return pool(f, [], [out], (130, 2 * cnt(out), 0, 0, 0))

    def dma(eng, f, rd, wr, nbytes, name):
        return add(eng, [f], regs(rd), regs(wr), 60.0, "dma", name, 1800.0 + nbytes / 250.0)

    def remote(srcs, dsts, name, nbytes):
        def f(q, T, c):
            trs = [RemoteDMATransfer(dst_ids=[DstId(rid=c["dst"][d][0], pnc=c["dst"][d][1])], dma_engine_mask=c["mask"][d],
                                     remote_sem=T.sem["a_" + name], src=ap(T, srcs[d]), dst=ap(T, dsts[d])) for d in range(2)]
            return q.remote_dma_fused(trs, local_sem=T.sem["s_" + name])
        i = add("pool", [f], regs(srcs), [], 400.0, "rem", "s_" + name, 1500.0 + nbytes / 200.0)
        return add("net", [], [], regs(dsts), 0.0, "arr", "a_" + name, 300.0, after=[i])

    dma("sp", lambda q, T, c: q.dma_start(T.X[:, 0:1024], T.feat[:, 0:1024]), [], [v("X", 0, 1024)], 262144, "l_x0")
    dma("act", lambda q, T, c: q.dma_start(T.H[:, 0:1024], T.hits[:, 0:1024]), [], [v("H", 0, 1024)], 524288, "l_h0")
    dma("sp", lambda q, T, c: q.dma_start(T.lane[:, :], T.lane0[:, :]), [], [v("lane", 0, 12)], 6144, "l_ln")
    dma("act", lambda q, T, c: q.dma_start(T.H[:, 1024:2048], T.hits[:, 1024:2048]), [], [v("H", 1024, 2048)], 1000000, "l_h1")
    dma("sp", lambda q, T, c: q.dma_start(T.X[:, 1024:2048], T.feat[:, 1024:2048]), [], [v("X", 1024, 2048)], 600000, "l_x1")
    dma("sp", lambda q, T, c: q.dma_start(T.th1[0:1, 0:8], T.th[:]), [], [v("th1", 0, 8)], 32, "l_th")
    iota(v("pc", 0), [[0, 1]], 0, 1)
    iota(v("J", 0, 160), [[1, 160]], 0, 0)
    iota(v("Jg", 0, 128), [[16, 8], [0, 16]], 0, 0)
    remote([v("X", 0, 1024)] * 2, [v("X", 2048, 3072), v("X", 3072, 4096)], "x", 524288)
    iota(v("NI", 0, 512), [[1, 512]], 0, 0)
    iota(v("NI", 512, 1024), [[1, 512]], 512, 0)
    C = lambda k: v("col", k)
    M = lambda n: v(n, 0, 128)
    V(ts(v("pc", 1), v("pc", 0), 15, AL.bitwise_and))
    V(cp(v("col", 0, 2), v("pc", 0, 2)))
    V(tt(C(2), C(0), C(1), AL.subtract))
    V(ts(C(3), C(2), 15.0, AL.add), ts(C(4), C(1), 2.0, AL.is_lt), ts(C(5), C(0), 16.0, AL.add))
    V(ts(v("LT", 0, 16), v("J", 0, 16), C(1), AL.is_gt), ts(v("EQ", 0, 16), v("J", 0, 16), C(1), AL.is_equal))
    V(ts(M("BO1"), M("Jg"), C(2), AL.is_equal))
    for r in range(16):
        V(ts(v("SELT", 128 * r, 128 * r + 128), M("BO1"), v("EQ", r), AL.mult))
        act(v("TRI", 128 * r, 128 * r + 128), M("BO1"), AF.Copy, scale=v("LT", r))
    J144 = v("J", 0, 144)
    V(ts(v("Z4", 0, 144), J144, C(3), AL.is_equal, 4096.0, AL.mult))
    V(ts(v("Z8", 0, 144), v("Z4", 0, 144), -2.0, AL.mult))
    V(ts(v("ZF", 0, 144), J144, C(3), AL.is_equal, C(4), AL.mult))
    for t, r in enumerate((0, 1, 2, 3, 4, 15)):
        V(ts(v("ZT", 144 * t, 144 * t + 144), J144, C(3), AL.is_equal, v("EQ", r), AL.mult))
    V(ts(M("I1"), M("J"), C(0), AL.is_equal))
    for n, w in (("IH", 0.5), ("IB", BIG), ("IM", -BIG), ("IN", 1.0), ("IX", -1.0), ("I4", 4096.0)):
        V(ts(M(n), M("I1"), w, AL.mult))
    V(ts(M("BO4"), M("BO1"), 4096.0, AL.mult))
    V(ts(M("BOF"), M("BO1"), C(4), AL.mult))
    V(ts(v("pc", 1), v("pc", 0), 16, AL.bitwise_and))
    V(ts(C(6), v("pc", 1), 0.0, AL.is_equal), ts(C(7), v("pc", 1), 0.0, AL.not_equal))
    V(ts(v("IW0", 0, 160), v("J", 0, 160), C(5), AL.is_equal, C(6), AL.mult))
    V(ts(v("IW1", 0, 160), v("J", 0, 160), C(5), AL.is_equal, C(7), AL.mult))
    V(mset(v("ONE", 0, 192), 1.0), mset(v("CQ", 0, 64), -0.25), mset(v("C128", 0, 64), 128.0), mset(v("RST", 0, 64), 0.0))
    V(mset(v("zS", 192, 208), 0.0), mset(v("nl", 192, 208), 0), mset(v("PB", 192, 208), 2048.0), mset(v("bR", 192, 208), 2048.0),
      mset(v("PB", 400, 416), 2048.0))
    V(mset(v("RST", 0, 64, 16), 4.0 * BIG))
    V(ts(C(8), v("EQ", 0), -BIG, AL.mult), ts(C(9), v("EQ", 1), 63488.0, AL.mult))
    V(ts(v("CK", 0, 64), v("ONE", 0, 64), C(8), AL.mult, C(9), AL.add))
    V(ts(v("dum", 0, 12), v("J", 0, 12), 16.0, AL.mult, C(1), AL.add))
    V(*([ts(v("slot", 2 * k, 2 * k + 2), v("dum", 0, 2), 32.0 * (k // 2), AL.add) for k in range(8)]
        + [ts(v("slot", 16, 18), v("dum", 0, 2), -1.0, AL.mult, -0.5, AL.add)]))
    V(ts(v("dum", 0, 12), v("dum", 0, 12), 4096.0, AL.add))
    pool(lambda q, T, c: q.partition_broadcast(T.thb[:, :], T.th1[0:1, :], 128), [v("th1", 0, 8)], [v("thb", 0, 8)], 180.0)
    V(tt(v("col", 16, 24), v("thb", 0, 8), v("Z4", 15, 143, 16), AL.mult))
    add("dve", [lambda q, T, c: q.tensor_reduce(T.col[:, 10:11], T.col[:, 16:24], AxisListType.X, AL.add)],
        [("col", 16, 24)], [("col", 10, 11)], (0, 64, 0, 0, 0))
    V(ts(C(11), C(10), 2048.0, AL.add))
    TH = C(11)
    V(ts(M("I32"), M("J"), C(0), AL.is_equal))
    for h in range(2):
        a, b, q = 512 * h, 512 * h + 512, v("qA%d" % h, 0, 512)
        V(cp(v("L", a, b), v("H", a, b)))
        act(v("TA", a, b), v("L", a, b), AF.Relu, bias=4194304.0, scale=-4096.0)
        P([mm(q, M("I32"), v("NI", a, b), True, False)], True)
        P([mm(q, M("I1"), v("TA", a, b), False, True)], True)
        V(tt(v("Y0", a, b), v("H", a, b), q, AL.min))
        act(v("Y1", a, b), v("Y0", a, b), AF.Identity, bias=2048.0)
        act(v("Y2", a, b), v("Y0", a, b), AF.Identity, bias=3072.0)
    remote([v("Y1", 0, 1024), v("Y2", 0, 1024)], [v("L", 2048, 3072), v("L", 3072, 4096)], "l", 1048576)
    iota(v("LO", 0, 256), [[0, 4], [1, 64]], 0, 0)
    for a in range(0, WT, 512):
        b = min(WT, a + 512)
        iota(v("FH", a, b), [[64, (b - a) // 64], [0, 64]], a - 2048, 0)
    dma("sp", lambda q, T, c: q.dma_start(T.FH[1:128:16, 0:4096], T.LO[:, :]), [v("LO", 0, 256)], [v("FH", 0, 4096)], 65536, "l_lo")

    Xw, Lw, Fw, Fo = v("X", 0, 4096), v("L", 0, 4096), v("FH", 0, 4096), v("FH", 0, 2048)
    XW, LW, FW = v("X", 0, WT), v("L", 0, WT), v("FH", 0, WT)
    XG, LG, FG = v("X", 2048, WT), v("L", 2048, WT), v("FH", 2048, WT)
    O = lambda k, n=12: v("o", 12 * k, 12 * k + n)
    seq = [0]

    def big(key, G, ch, w, U):
        for h in range(2):
            gather(eng_of(key + (ch, h), "act"), v(G, 1024 * ch + 512 * h, 1024 * ch + 512 * h + 512), w,
                   v(U, CL * ch + 32 * h, CL * ch + 32 * h + 32))

    def names(t, ch, lU, xU, xN):
        a, b = CL * ch, CL * ch + CL
        if t == 0:
            V(ts(v(xN, a, b), v(lU, a, b), -2048.0, AL.add))
            return lU
        f0 = 1024 * ch
        big((t, "F" + xU), "Fg", ch, Fw, lU)
        q = v("qP", 384 + 64 * (seq[0] % 2), 448 + 64 * (seq[0] % 2))
        seq[0] += 1
        P([mm(q, zs("ZF", k), v("Fg", f0 + k, f0 + 1024, 16), k == 0, k == 15) for k in range(16)])
        V(ts(v(xU, a, b), q, 2048.0, AL.add))
        V(ts(v(xN, a, b), v(xU, a, b), -2048.0, AL.add))
        return xU

    def dist(t, q, A, G, ch, yP, y, first, last):
        f0 = 1024 * ch
        blk = lambda k: v(A, f0 + 64 * k, f0 + 64 * k + 64)
        if eng_of((t, A, ch), "dve") == "dve":
            for k0 in (0, 8):
                V(*[tt(blk(k), v(G, f0 + k, f0 + 1024, 16), yP, AL.min) for k in range(k0, k0 + 8)])
            if A != "A3" and eng_of((t, "A1", ch), "dve") == eng_of((t, "A2", ch), "dve") == "dve" and eng_of((t, "sg", ch), "act") == "dve":
                sN = v("sN", CL * ch, CL * ch + CL)
                if A == "A1":
                    sq = v("qR", 384 + 64 * (ch % 2), 448 + 64 * (ch % 2))
                    P([mm(sq, zs("Z4", k), v(G, f0 + k, f0 + 1024, 16), k == 0, k == 15) for k in range(16)])
                    V(ts(sN, sq, 1.0 / 4096, AL.mult, -2048.0, AL.add))
                P([mm(q, M("I4"), sN, True, False), mm(q, M("BO4"), v("C128", 0, 64), False, False)], True)
            else:
                P([mm(q, zs("Z4", k), v(G, f0 + k, f0 + 1024, 16), k == 0, False) for k in range(16)], True)
            P([mm(q, M("BO4"), y, False, False)] + [mm(q, l, r, False, False) for l, r in first[:1]], True)
            for k0 in (0, 8):
                P([mm(q, zs("Z8", k), blk(k), False, False) for k in range(k0, k0 + 8)], True)
            first = first[1:]
        else:
            for k0 in (0, 8):
                bk = "qA%d" % (k0 // 8)
                P([x for k in range(8) for x in (mm(v(bk, 64 * k, 64 * k + 64), M("I1"), v(G, f0 + k0 + k, f0 + 1024, 16), True, False),
                                                 mm(v(bk, 64 * k, 64 * k + 64), M("IX"), y, False, True))])
                act(v(A, f0 + 64 * k0, f0 + 64 * k0 + 512), v(bk, 0, 512), AF.Abs)
                P([mm(q, zs("Z4", k), blk(k), k == 0, False) for k in range(k0, k0 + 8)], True)
        last = first + last
        P([mm(q, l, r, False, i == len(last) - 1) for i, (l, r) in enumerate(last)], True)

    late = []
    for t in range(RO):
        par = t % 2
        last = t == RO - 1
        pU = lambda a=0, b=12: v("PAR", 12 * t + a, 12 * t + b)
        pI = v("pI", 12 * par, 12 * par + 12)
        pb = 208 * par
        pR = lambda a=0, b=192: v("qP", 192 * par + a, 192 * par + b)
        pHL = v("pHL", 192 * par, 192 * par + 192)
        fl = lambda k, ch: v("fl", 192 * k + CL * ch, 192 * k + CL * ch + CL)
        if t == 0:
            V(cp(pU(), v("lane", 0, 12)))
            V(cp(pI, v("lane", 0, 12)), ts(v("oR", 48, 60), v("lane", 0, 12), -2048.0, AL.add))
            spread("qP", 0, v("oR", 48, 60), 12)
            act(v("PB", pb, pb + 192), pR(), AF.Identity, bias=2048.0)
        src0 = v("H", 0, 2048) if t == 0 else v("L", 0, 2048)
        for ch in range(NCH):
            V(cp(v("lvU", CL * ch, CL * ch + CL), ind(src0, pU(4 * ch, 4 * ch + 4))))
        gather(eng_of((t, "xv"), "act"), v("xv", 0, 192), v("X", 0, 2048), pU())
        P([mm(v("qZ", 0, 192), M("I1"), v("xv", 0, 192), True, True)])
        if t == 0:
            for h in (2, 3):
                V(cp(v("L", 512 * h, 512 * h + 512), v("H", 512 * h, 512 * h + 512)))
        for f in late:
            f()
        late = []
        for ch in range(NCH):
            a, b = CL * ch, CL * ch + CL
            big((t, "Gc"), "Gc", ch, Xw, names(t, ch, "lvU", "cU", "cN"))
            V(tt(fl(0, ch), v("cN", a, b), pR(a, b), AL.is_equal))
            q = v("qK%d" % (ch % 2), 256 + a, 256 + b)
            dist(t, q, "A1", "Gc", ch, v("qZ", a, b), v("xv", a, b), [], [(M("IB"), fl(0, ch)), (M("IN"), v("cN", a, b))])
            V(tr(v("KT", a, b), q))
            V(scan(v("KS", a, b), v("RST", 0, 64), v("KT", a, b), 0.0, AL.add, AL.min))
            V(ts(fl(1, ch), q, TH, AL.is_ge, -4096.0, AL.mult))
            V(ts(v("KI", a, b), v("KS", a, b), 2048.0 - BIG, AL.add))
            V(ts(v("KI", 192 + a, 192 + b), v("KI", a, b), 4095, AL.bitwise_and))
            V(cp(v("KS", a, b), v("KI", 192 + a, 192 + b)))
            P([mm(v("qS", 4 * ch + h2, 4 * ch + 4, 2), v("IW%d" % h2, 16 - 16 * (h - h2), 144 - 16 * (h - h2)),
                  v("KS", a + 16 * h + 15, b, 32), h == 0, h == 1) for h2 in range(2) for h in range(2)])
            V(tr(v("bR", a, b), v("KS", a, b)))
            bU = v("sU", 4 * ch, 4 * ch + 4)
            V(cp(bU, v("qS", 4 * ch, 4 * ch + 4)))
            V(cp(v("lbU", a, b), ind(Lw, bU)))
            gather(eng_of((t, "xb", ch), "act"), v("xb", a, b), Xw, bU)
            zq = v("qZ", 384 + 64 * (ch % 2), 448 + 64 * (ch % 2))
            P([mm(zq, M("IH"), v("xv", a, b), True, False), mm(zq, M("I1"), v("CQ", 0, 64), False, False),
               mm(zq, M("IH"), v("xb", a, b), False, True)])
            V(ts(v("zS", a, b), zq, 12582912.0, AL.add, -12582912.0, AL.add))
            P([mm(v("qZ", 192 + a, 192 + b), M("I1"), v("zS", a, b), True, True)])
        for q0, q1 in ((0, 3), (3, 7), (7, 12)):
            V(*[ts(v("E", 208 * q, 192 * q + 192), v("PB", pb + 16 * q, pb + 192), v("pI", 12 * par + q), AL.is_equal)
                for q in range(q0, q1)])
        P([mm(v("qS", 128, 320), M("TRI"), v("E", 0, 192), True, False)]
          + [mm(v("qS", 144 + 16 * q, 320), M("BO1"), v("E", 208 * q + 16, 192 * q + 192), False, False) for q in range(11)]
          + [mm(v("qS", 128 + r, 320, 16), v("TRI", 128 * r, 128 * r + 128), v("E", r, 2304, 208), False, r == 15) for r in range(1, 16)])
        V(ts(v("cN", 192, 384), v("qS", 128, 320), 0.0, AL.not_equal))
        diag(v("qS", 12, 36), "ZT", "cN", 0, 384, 144 * t)
        ct, na = v("qS", 12, 24), v("qS", 24, 36)
        V(tt(O(0), na, v("dum", 0, 12), AL.mult), ts(O(1), na, -1.0, AL.mult, 1.0, AL.add), ts(O(2), pI, -2048.0, AL.add))
        V(tt(O(3), O(0), pI, AL.max))
        V(cp(v("sU", 12, 24), O(3)))
        aw, pn = O(1), O(2)
        bI = v("qS", 0, 12)
        V(ts(v("sU", 24, 36), bI, 2047.0, AL.min))
        if t == 0:
            dma("sp", lambda q, T, c: q.dma_start(T.H[15:128:16, 0:2048], T.hits[0:128:16, :]), [], [v("H", 0, 2048)], 65536, "l_b")
        for ch in range(NCH):
            V(cp(ind(v("H", 0, 4320), v("sU", 12 + 4 * ch, 16 + 4 * ch)), v("bR", CL * ch, CL * ch + CL)))
        V(ts(v("BgN", 0, 192), ind(v("H", 0, 2048), v("sU", 24, 36)), -2048.0, AL.add))
        back = v("qS", 48, 60)
        diag(back, "ZT", "BgN", 0, 192, 144 * 5)
        if t > 0:
            V(ts(v("sU", 36, 48), back, 2048.0, AL.add))
            gather(eng_of((t, "bk"), "dve"), v("bk", 0, 192), Fw, v("sU", 36, 48))
            back = v("qS", 36, 48)
            diag(back, "ZF", "bk", 0, 192)
        e, own, j = O(4), O(5), O(11)
        V(tt(e, bI, pI, AL.subtract), ts(own, bI, 2048.0, AL.is_lt), ts(O(6), bI, 2048.0, AL.add), ts(O(23), pI, 1024.0, AL.is_lt))
        V(tt(O(7), bI, O(3), AL.is_gt))
        V(tt(O(9), O(7), own, AL.mult))
        V(tt(O(10), back, pn, AL.is_equal))
        V(tt(j, O(10), O(9), AL.mult))
        V(tt(O(12), j, O(6), AL.mult), ts(O(26), j, -1.0, AL.mult, 1.0, AL.add), *([] if last else [tt(v("oR", 24, 36), j, O(23), AL.mult)]))
        V(ts(v("oR", 12, 24), O(12), -4096.0, AL.add), tt(O(13), O(26), v("dum", 0, 12), AL.mult))
        spread("qR", 0, v("oR", 12, 24 if last else 36), 12 if last else 24)
        act(v("fl", 192 * 2, 192 * 3), v("qR", 0, 192), AF.Relu, bias=-4095.0, scale=-1.0)
        lg = 36 * t
        V(tt(O(20), O(13), pI, AL.max), tt(O(22), O(13), bI, AL.max))
        if not last:
            V(ts(O(14), ct, 0.0, AL.is_lt), tt(O(15), ct, pn, AL.subtract))
            V(tt(O(16), O(14), O(15), AL.mult))
            V(tt(O(17), e, O(16), AL.subtract))
            V(tt(O(18), O(17), own, AL.mult))
            V(tt(O(19), O(18), O(16), AL.add))
            V(tt(O(24), aw, j, AL.subtract))
            V(tt(O(25), O(19), O(24), AL.mult))
            V(tt(O(21), O(25), pI, AL.add))
            V(cp(v("LOG", lg, lg + 36), O(20, 36)))
            V(scan(v("cS", 0, 192), v("ONE", 0, 192), v("qR", 192, 384), 0.0, AL.mult, AL.add))
            for k in range(2):
                if eng_of((t, "sn", k), "act") == "act":
                    act(v("junk", 0, 192), v("cS", 0, 192), AF.Sign, bias=v("slot", 16 + k), acc=v("col", 12 + k))
                    V(ts(v("sU", 48 + k), v("col", 12 + k), -0.5, AL.mult, 96.0, AL.add))
                else:
                    V(ts(v("jk", 0, 192), v("cS", 0, 192), v("slot", k), AL.is_le))
                    V(scan(v("jk", 192, 384), v("ONE", 0, 192), v("jk", 0, 192), 0.0, AL.mult, AL.add))
                    V(cp(v("sU", 48 + k), v("jk", 383)))
            sel = v("sU", 48, 50)
            V(ts(v("vbN", 0, 32), ind(v("PB", pb, pb + 208), sel), -2048.0, AL.add), ts(v("vbN", 32, 64), ind(v("bR", 0, 208), sel), -2048.0, AL.add))
            m1 = 36 * t
            V(cp(v("M1", m1, m1 + 32), ind(v("zS", 0, 208), sel)))
            diag(v("qS", 60, 64), "ZT", "vbN", 0, 64, 144 * 5)
            V(ts(v("m", 128, 132), v("qS", 60, 64), -1024.0, AL.is_ge, 8192.0, AL.mult))
            V(tt(v("m", 132, 136), v("m", 128, 132), v("qS", 60, 64), AL.add))
            V(tt(v("M1", m1 + 32, m1 + 36), v("m", 132, 136), v("slot", 4 * t, 4 * t + 4), AL.min))
            remote([v("M1", m1, m1 + 36)] * 2, [v("LA1", 72 * t, 72 * t + 36), v("LA1", 72 * t + 36, 72 * t + 72)], "m%d" % t, 36864)
            V(cp(v("m", 0, 32), ind(v("PB", pb, pb + 208), sel)))
        else:
            V(cp(v("LOG", lg, lg + 12), O(20)), cp(v("LOG", lg + 24, lg + 36), O(22)))
        if t == 0:
            gather("act", pHL, Fw, pU())
        ous = [names(t, ch, "lbU", "oU", "oN") for ch in range(NCH)]
        V(cp(ind(FW, v("LOG", lg + 24, lg + 36)), pHL))
        if not last:
            n2 = 1 - par
            nH = v("pHL", 192 * n2, 192 * n2 + 192)
            gather(eng_of((t, "to"), "dve"), nH, Fo, v("LOG", lg + 12, lg + 24))
            diag(v("qS", 64, 76), "ZF", "pHL", 192 * n2, 192)
            V(ts(v("PAR", 12 * t + 12, 12 * t + 24), v("qS", 64, 76), 2048.0, AL.add),
              ts(v("pI", 12 * n2, 12 * n2 + 12), v("qS", 64, 76), 2048.0, AL.add))
            P([mm(v("qP", 192 * n2, 192 * n2 + 192), M("BOF"), nH, True, True)])
            act(v("PB", 208 * n2, 208 * n2 + 192), v("qP", 192 * n2, 192 * n2 + 192), AF.Identity, bias=2048.0)
            for s in range(t):
                gather(eng_of((t, "cg", s), "act"), v("CG", 192 * s, 192 * s + 192), Fo, v("PAR", 12 * s, 12 * s + 12))
            for s in range(t):
                V(cp(ind(FW, v("LOG", 36 * s + 24, 36 * s + 36)), v("CG", 192 * s, 192 * s + 192)))
            la = 72 * t
            for d in range(2):
                V(ts(v("GP", 4 * t + 2 * d, 4 * t + 2 * d + 2), v("LA1", la + 36 * d + 32, la + 36 * d + 34), 2048.0 + 1024 * d, AL.add),
                  ts(v("GJ", 4 * t + 2 * d, 4 * t + 2 * d + 2), v("LA1", la + 36 * d + 34, la + 36 * d + 36), 2048.0 + 1024 * d, AL.add))
            V(cp(v("GH", 0, 64), ind(FG, v("GP", 4 * t, 4 * t + 4))))
            V(cp(ind(FG, v("GJ", 4 * t, 4 * t + 4)), v("GH", 0, 64)))
            if t > 0:
                V(cp(v("CG", 192 * t, 256 * t), ind(FG, v("GP", 0, 4 * t))))
                V(cp(ind(FG, v("GJ", 0, 4 * t)), v("CG", 192 * t, 256 * t)))
            if 0 < t < RO - 2:
                diag(v("qS", 76, 76 + 16 * t), "ZF", "CG", 0, 256 * t)
                V(ts(v("PAR", 0, 12 * t), v("qS", 76, 76 + 12 * t), 2048.0, AL.add),
                  ts(v("GP", 0, 4 * t), v("qS", 76 + 12 * t, 76 + 16 * t), 2047.0, AL.min))
        else:
            diag(v("qR", 384, 512), "ZF", "FH", 0, 2048)
            V(ts(v("FU", 0, 128), v("qR", 384, 512), 2048.0, AL.add))
            for h in range(4):
                gather(eng_of((t, "fu", h), "act"), v("FT", 512 * h, 512 * h + 512), Fo, v("FU", 32 * h, 32 * h + 32))
                q = v("qA%d" % (h % 2), 0, 512, 1, (0, 8))
                P([mm(q, v("ZF", 15, 143, 16), v("FT", 512 * h, 512 * h + 512), True, True)])
                act(v("YF", 512 * h, 512 * h + 512, 1, (0, 8)), q, AF.Identity, bias=2048.0)
            dma("sp", lambda q, T, c: q.dma_start(T.yf[:, :], T.YF[0:8, :]), [v("YF", 0, 2048)], [], 65536, "o_f")
        for ch in range(NCH):
            big((t, "Go"), "Go", ch, Xw, ous[ch])
        V(cp(ind(XW, v("LOG", lg, lg + 12)), v("zS", 0, 192)))
        if not last:
            for d in range(2):
                V(cp(ind(XG, v("GP", 4 * t + 2 * d, 4 * t + 2 * d + 2)), v("LA1", la + 36 * d, la + 36 * d + 32)))
        else:
            dma("sp", lambda q, T, c: q.dma_start(T.yx[:, :], T.X[:, 0:2048]), [v("X", 0, 2048)], [], 524288, "o_x")
        for ch in range(NCH):
            a, b = CL * ch, CL * ch + CL
            zP, zS = v("qZ", 192 + a, 192 + b), v("zS", a, b)
            IB, ck = M("IB"), [(M("BO1"), v("CK", 0, 64))]
            V(tt(fl(3, ch), v("cN", a, b), v("qR", a, b), AL.is_equal), tt(fl(4, ch), fl(1, ch), v("qR", a, b), AL.is_equal))
            V(tt(fl(5, ch), v("oN", a, b), v("qR", a, b), AL.is_equal))
            V(tt(fl(6, ch), v("oN", a, b), pR(a, b), AL.is_equal))
            kc, ko = v("qK0", a, b), v("qK1", a, b)
            dist(t, kc, "A2", "Gc", ch, zP, zS, ck, [(IB, fl(0, ch)), (IB, fl(3, ch)), (IB, fl(4, ch)), (M("IN"), v("cN", a, b))])
            V(tt(v("t1", a, b), kc, v("PB", pb + a, pb + b), AL.min))
            dist(t, ko, "A3", "Go", ch, zP, zS, ck + [(IB, fl(2, ch)), (M("IM"), fl(4, ch)), (IB, fl(5, ch)), (IB, fl(6, ch))],
                 [(M("IN"), v("oN", a, b))])
            V(tt(v("n0", a, b), ko, v("t1", a, b), AL.min))
            V(ts(v("nl", a, b), v("n0", a, b), 4095, AL.bitwise_and))
            V(cp(ind(LW, v("sU", 12 + 4 * ch, 16 + 4 * ch)), v("nl", a, b)))
        if last:
            dma("sp", lambda q, T, c: q.dma_start(T.yl[:, :], T.L[:, 0:2048]), [v("L", 0, 2048)], [], 1048576, "o_l")
        else:
            def second(t=t, sel=sel):
                nw = ind(v("nl", 0, 208), sel)
                V(ts(v("m", 32, 64), nw, 1024.0, AL.is_lt, 4096.0, AL.mult))
                V(tt(v("m", 64, 96), v("m", 32, 64), v("m", 0, 32), AL.add))
                V(tt(v("M2", 32 * t, 32 * t + 32), nw, v("m", 64, 96), AL.min))
                remote([v("M2", 32 * t, 32 * t + 32)] * 2, [v("LA2", 64 * t, 64 * t + 32), v("LA2", 64 * t + 32, 64 * t + 64)], "n%d" % t, 32768)
                for d in range(2):
                    V(ts(ind(LG, v("GP", 4 * t + 2 * d, 4 * t + 2 * d + 2)), v("LA2", 64 * t + 32 * d, 64 * t + 32 * d + 32),
                         1.0, AL.mult, 2048.0 + 1024 * d, AL.add))
            late = [second]
    return ops


def times(ops, m):
    return ([sum(a * b * (m[1] if k in (2, 3) else 1.0) for k, (a, b) in enumerate(zip(o["dur"], m))) for o in ops],
            [o["lat"] * m[7] for o in ops])


def one_pass(ops, dur, lat, pre, prio, m, back):
    n = len(ops)
    deps = [set(d) for d in pre]
    succ = [[] for _ in ops]
    for i in range(n):
        for d in pre[i]:
            succ[d].append(i)
    left = [len(d) for d in pre]
    eng = [o["eng"] for o in ops]
    comp = [o["kind"] == "c" for o in ops]
    ready = {e: {} for e in ENG + ("net",)}
    free = {e: 0.0 for e in ready}
    fin, start, bank, order = [0.0] * n, [0.0] * n, {}, []
    for i in range(n):
        if left[i] == 0:
            ready[eng[i]][i] = lat[i] if back else 0.0
    while len(order) < n:
        best = None
        for e in ready:
            if ready[e]:
                cand = []
                for i, s in ready[e].items():
                    s = max(s, free[e])
                    for b in ops[i]["banks"]:
                        for e2, d in bank.get(b, {}).items():
                            if e2 != e and fin[d] + m[5] > s:
                                s = fin[d] + m[5]
                    cand.append((s, i))
                s0 = min(cand)[0]
                if best is None or s0 < best[0]:
                    best = (s0, e, cand)
        s0, e0, cand = best
        s, i = max([c for c in cand if c[0] <= s0 + SLACK], key=lambda c: (prio[c[1]], -c[1]))
        for b in ops[i]["banks"]:
            deps[i] |= set(d for e, d in bank.get(b, {}).items() if e != e0)
            bank.setdefault(b, {})[e0] = i
        start[i], free[e0] = s, s + dur[i]
        fin[i] = s + dur[i] + (0.0 if back else lat[i])
        del ready[e0][i]
        order.append(i)
        for k in succ[i]:
            left[k] -= 1
            if left[k] == 0:
                ready[eng[k]][k] = (lat[k] if back else 0.0) + max(
                    fin[d] + ((0.0 if eng[k] == "pe" else m[6]) if eng[d] == eng[k] and comp[k if back else d] else m[5]) for d in pre[k])
    return {"order": order, "deps": deps, "start": start, "fin": fin, "dur": dur}


def schedule(ops, noise, m=MODEL, turns=2):
    n = len(ops)
    dur, lat = times(ops, m)
    pre = [o["deps"] for o in ops]
    post = [set() for _ in ops]
    for i in range(n):
        for d in pre[i]:
            post[d].add(i)
    prio = [0.0] * n
    for i in range(n - 1, -1, -1):
        prio[i] = dur[i] + lat[i] + max([prio[s] + m[5] for s in post[i]] + [0.0])
    best = plan = one_pass(ops, dur, lat, pre, [p + noise.get(i, 0.0) for i, p in enumerate(prio)], m, False)
    for _ in range(turns):
        rev = one_pass(ops, dur, lat, post, plan["fin"], m, True)
        plan = one_pass(ops, dur, lat, pre, [p + noise.get(i, 0.0) for i, p in enumerate(rev["fin"])], m, False)
        if max(plan["fin"]) < max(best["fin"]):
            best = plan
    return best


def place_waits(ops, plan):
    order, fin = plan["order"], plan["fin"]
    pos, num = {}, {e: 0 for e in ENG}
    know = {e: ({x: 0 for x in ENG}, set()) for e in ENG}
    snap, waits, needed = {}, {}, set()
    for i in order:
        e = ops[i]["eng"]
        if e == "net":
            snap[i] = ({x: 0 for x in ENG}, set())
            continue
        clock, seen = know[e]
        w = []
        for d in sorted(plan["deps"][i], key=lambda d: (-fin[d], d)):
            p = ops[d]
            if p["kind"] == "c":
                if (p["eng"] == e == "pe") or clock[p["eng"]] >= pos[d]:
                    continue
                clock[p["eng"]] = pos[d]
            else:
                if d in seen:
                    continue
                seen.add(d)
            w.append(d)
            needed.add(d)
            for x in ENG:
                clock[x] = max(clock[x], snap[d][0][x])
            seen.update(snap[d][1])
        waits[i] = w
        num[e] += 1
        pos[i] = num[e]
        snap[i] = (dict(clock), set(seen))
    for e in ENG:
        mine = [i for i in order if ops[i]["eng"] == e and ops[i]["kind"] == "c"]
        if mine:
            needed.add(mine[-1])
    count, tot = {}, {e: 0 for e in ENG}
    for i in order:
        if ops[i]["kind"] == "c" and i in needed:
            tot[ops[i]["eng"]] += 1
            count[i] = tot[ops[i]["eng"]]
    plan.update({"waits": waits, "count": count, "tot": tot})
    return plan


OPS = build(CFG)
PLAN = place_waits(OPS, schedule(OPS, NOISE))
SEMAPHORES = ["c_" + e for e in ENG if PLAN["tot"][e]] + [o["sem"] for o in OPS if o["sem"]]


def rank_program(g, core, T, topo):
    rank = T.rank_of(core)
    if rank is None:
        return
    n = len(T.cores)
    dsts = [T.cores[(rank - d) % n] for d in (1, 2)]
    masks, out, arr = [], 0, 0
    for d in range(2):
        en = topo.engines(core, dsts[d])
        h = len(en) // 2
        masks.append(sum(1 << e for e in en[d * h:(d + 1) * h]))
        out += h
        arr += len(topo.engines(T.cores[(rank + d + 1) % n], core)) // 2
    c = {"dst": [topo.addr(x)[:2] for x in dsts], "mask": masks}
    Q = {"pe": g.tensor, "dve": g.vector, "act": g.scalar, "pool": g, "sp": g.sync}

    def sem_of(d):
        o = OPS[d]
        if o["kind"] == "c":
            return T.sem["c_" + o["eng"]], PLAN["count"][d]
        return T.sem[o["sem"]], {"dma": 16, "rem": out, "arr": arr}[o["kind"]]
    for i in PLAN["order"]:
        o = OPS[i]
        if o["eng"] == "net":
            continue
        q = Q[o["eng"]]
        for d in PLAN["waits"][i]:
            q.wait_ge(*sem_of(d))
        for f in o["ins"]:
            r = f(q, T, c)
        if o["kind"] == "dma":
            r.then_inc(T.sem[o["sem"]], 16)
        elif i in PLAN["count"]:
            r.then_inc(T.sem["c_" + o["eng"]], 1)
    for e in ENG:
        if PLAN["tot"][e]:
            g.wait_ge(T.sem["c_" + e], PLAN["tot"][e])
    for i, o in enumerate(OPS):
        if o["sem"]:
            g.wait_ge(*sem_of(i))
